import numpy as np
import ml_dtypes

BF16 = ml_dtypes.bfloat16


def bf(x):
    return np.asarray(x, np.float32).astype(BF16)


def f32(x):
    return np.asarray(x, np.float32)


def f64(x):
    return np.asarray(x).astype(np.float64)


def striped(idx):
    return np.tile(idx.reshape(-1, 16).T, (8, 1))


S, K, M, N, E, Q = 512, 128, 512, 512, 2, 256


def setup_inputs():
    return {"base": bf(np.random.standard_normal((M, S))), "x": bf(np.random.standard_normal((K, N))), "w": bf(np.random.standard_normal((E, K, M)) / np.sqrt(K)), "c": f32(0.2 + 0.8 * np.random.random_sample((1, S))), "offs": striped(np.random.permutation(S))}


def reference(base, x, w, c, offs):
    idx = offs[:16].T.reshape(-1)
    z = f64(base).copy()
    for e in range(E):
        z[:, idx[e * Q : (e + 1) * Q]] += f64(w)[e].T @ f64(x)[:, e * Q : (e + 1) * Q]
    return z * f64(c)

@@ -1,0 +1,53 @@
+import concourse.mybir as mybir
+from concourse.masks import make_identity
+
+BF16, F32, U16 = mybir.dt.bfloat16, mybir.dt.float32, mybir.dt.uint16
+P = 128
+FLOPS = 2 * 128 * 512 * 512 + 2 * 512 * 512
+
+
+def tile_scatter_matmul_kernel(tc, base, x, w, c, offs, out):
+    nc = tc.nc
+    M, S = base.shape
+    K, N = x.shape
+    E = w.shape[0]
+    Q = N // E
+    blocks = M // P
+
+    with (
+        tc.tile_pool(name="held", bufs=1) as held,
+        tc.psum_pool(name="psum", bufs=1) as psum,
+    ):
+        offsets = held.tile([P, N // 16], U16, name="offsets")
+        base_tile = held.tile([P, blocks, S], BF16, name="base_tile")
+        x_tile = held.tile([K, N], BF16, name="x_tile")
+        w_tile = held.tile([K, E, M], BF16, name="w_tile")
+        c_tile = held.tile([P, S], F32, name="c_tile")
+        ident = held.tile([P, P], BF16, name="ident")
+
+        nc.sync.dma_start(base_tile[:], base.rearrange("(a p) t -> p a t", p=P))
+        nc.sync.dma_start(offsets[:], offs)
+        nc.sync.dma_start(w_tile[:], w.rearrange("e k m -> k e m"))
+        nc.sync.dma_start(x_tile[:], x)
+        nc.sync.dma_start(c_tile[:], c.rearrange("o t -> (o t)").partition_broadcast(P))
+        make_identity(nc, ident[:])
+
+        windows = [psum.tile([P, S], F32, name=f"window{a}") for a in range(blocks)]
+        for a in range(blocks):
+            nc.tensor.matmul(windows[a][:], ident[:], base_tile[:, a, :], start=True, stop=False)
+
+        for a in range(blocks):
+            for e in range(E):
+                piece = offsets[:, e * Q // 16 : (e + 1) * Q // 16]
+                nc.tensor.matmul(
+                    windows[a][:].indirect(piece),
+                    w_tile[:, e, a * P : (a + 1) * P],
+                    x_tile[:, e * Q : (e + 1) * Q],
+                    start=False,
+                    stop=(e == E - 1),
+                )
+
+        for a in range(blocks):
+            result = held.tile([P, S], F32, name=f"result{a}")
+            nc.vector.tensor_tensor(result[:], windows[a][:], c_tile[:], mybir.AluOpType.mult)
+            nc.sync.dma_start(out[a * P : (a + 1) * P, :], result[:])

@@ -19,22 +19,30 @@ def tile_scatter_matmul_kernel(tc, base, x, w, c, offs, out):
         tc.psum_pool(name="psum", bufs=1) as psum,
     ):
         offsets = held.tile([P, N // 16], U16, name="offsets")
-        base_tile = held.tile([P, blocks, S], BF16, name="base_tile")
+        halves = [held.tile([P, blocks // 2, S], BF16, name=f"half{h}") for h in range(2)]
         x_tile = held.tile([K, N], BF16, name="x_tile")
         w_tile = held.tile([K, E, M], BF16, name="w_tile")
         c_tile = held.tile([P, S], F32, name="c_tile")
+        zeros = held.tile([P, S], BF16, name="zeros")
         ident = held.tile([P, P], BF16, name="ident")
 
-        nc.sync.dma_start(base_tile[:], base.rearrange("(a p) t -> p a t", p=P))
+        base_blocks = base.rearrange("(h a p) t -> h p a t", h=2, p=P)
+        for h in range(2):
+            nc.sync.dma_start(halves[h][:], base_blocks[h])
         nc.sync.dma_start(offsets[:], offs)
         nc.sync.dma_start(w_tile[:], w.rearrange("e k m -> k e m"))
         nc.sync.dma_start(x_tile[:], x)
         nc.sync.dma_start(c_tile[:], c.rearrange("o t -> (o t)").partition_broadcast(P))
         make_identity(nc, ident[:])
+        nc.vector.memset(zeros[:], 0.0)
+
+        idle_bank = psum.tile([P, S], F32, name="idle_bank")
+        for step in range(4):
+            nc.tensor.matmul(idle_bank[:], zeros[:, :P], zeros[:], start=True, stop=True)
 
         windows = [psum.tile([P, S], F32, name=f"window{a}") for a in range(blocks)]
         for a in range(blocks):
-            nc.tensor.matmul(windows[a][:], ident[:], base_tile[:, a, :], start=True, stop=False)
+            nc.tensor.matmul(windows[a][:], ident[:], halves[a // 2][:, a % 2, :], start=True, stop=False)
 
         for a in range(blocks):
             for e in range(E):

@@ -26,13 +26,13 @@ def tile_scatter_matmul_kernel(tc, base, x, w, c, offs, out):
         zeros = held.tile([P, S], BF16, name="zeros")
         ident = held.tile([P, P], BF16, name="ident")
 
+        nc.scalar.dma_start(c_tile[:], c.rearrange("o t -> (o t)").partition_broadcast(P))
         base_blocks = base.rearrange("(h a p) t -> h p a t", h=2, p=P)
         for h in range(2):
             nc.sync.dma_start(halves[h][:], base_blocks[h])
         nc.sync.dma_start(offsets[:], offs)
         nc.sync.dma_start(w_tile[:], w.rearrange("e k m -> k e m"))
         nc.sync.dma_start(x_tile[:], x)
-        nc.sync.dma_start(c_tile[:], c.rearrange("o t -> (o t)").partition_broadcast(P))
         make_identity(nc, ident[:])
         nc.vector.memset(zeros[:], 0.0)
 

@@ -3,6 +3,7 @@ from concourse.masks import make_identity
 
 BF16, F32, U16 = mybir.dt.bfloat16, mybir.dt.float32, mybir.dt.uint16
 P = 128
+SQ = 32
 FLOPS = 2 * 128 * 512 * 512 + 2 * 512 * 512
 
 
@@ -22,11 +23,16 @@ def tile_scatter_matmul_kernel(tc, base, x, w, c, offs, out):
         halves = [held.tile([P, blocks // 2, S], BF16, name=f"half{h}") for h in range(2)]
         x_tile = held.tile([K, N], BF16, name="x_tile")
         w_tile = held.tile([K, E, M], BF16, name="w_tile")
+        c_cols = held.tile([P, S // SQ], F32, name="c_cols")
+        c_blocks = held.tile([P, S // SQ, SQ], F32, name="c_blocks", align_bytes=64)
+        c_flipped = held.tile([P, S], F32, name="c_flipped", align_bytes=64)
         c_tile = held.tile([P, S], F32, name="c_tile")
         zeros = held.tile([P, S], BF16, name="zeros")
         ident = held.tile([P, P], BF16, name="ident")
 
-        nc.scalar.dma_start(c_tile[:], c.rearrange("o t -> (o t)").partition_broadcast(P))
+        for g in range(P // SQ):
+            queue = nc.scalar if g % 2 == 0 else nc.sync
+            queue.dma_start(c_cols[g * SQ : (g + 1) * SQ, :], c.rearrange("o (q b) -> (o q) b", q=SQ))
         base_blocks = base.rearrange("(h a p) t -> h p a t", h=2, p=P)
         for h in range(2):
             nc.sync.dma_start(halves[h][:], base_blocks[h])
@@ -39,6 +45,12 @@ def tile_scatter_matmul_kernel(tc, base, x, w, c, offs, out):
         idle_bank = psum.tile([P, S], F32, name="idle_bank")
         for step in range(4):
             nc.tensor.matmul(idle_bank[:], zeros[:, :P], zeros[:], start=True, stop=True)
+
+        nc.vector.tensor_copy(c_blocks[:], c_cols[:].unsqueeze(2).to_broadcast([P, S // SQ, SQ]))
+        nc.vector.transpose(c_flipped[:], c_blocks[:].rearrange("p b q -> p (b q)"))
+        nc.vector.tensor_copy(
+            c_tile[:].rearrange("p (q b) -> p q b", q=SQ), c_flipped[:].rearrange("p (b q) -> p q b", q=SQ)
+        )
 
         windows = [psum.tile([P, S], F32, name=f"window{a}") for a in range(blocks)]
         for a in range(blocks):

import concourse.mybir as mybir
from concourse.masks import make_identity

BF16, F32, U16 = mybir.dt.bfloat16, mybir.dt.float32, mybir.dt.uint16
P = 128
SQ = 32
FLOPS = 2 * 128 * 512 * 512 + 2 * 512 * 512


def tile_scatter_matmul_kernel(tc, base, x, w, c, offs, out):
    nc = tc.nc
    M, S = base.shape
    K, N = x.shape
    E = w.shape[0]
    Q = N // E
    blocks = M // P

    with (
        tc.tile_pool(name="held", bufs=1) as held,
        tc.psum_pool(name="psum", bufs=1) as psum,
    ):
        offsets = held.tile([P, N // 16], U16, name="offsets")
        halves = [held.tile([P, blocks // 2, S], BF16, name=f"half{h}") for h in range(2)]
        x_tile = held.tile([K, N], BF16, name="x_tile")
        w_tile = held.tile([K, E, M], BF16, name="w_tile")
        c_cols = held.tile([P, S // SQ], F32, name="c_cols")
        c_blocks = held.tile([P, S // SQ, SQ], F32, name="c_blocks", align_bytes=64)
        c_flipped = held.tile([P, S], F32, name="c_flipped", align_bytes=64)
        c_tile = held.tile([P, S], F32, name="c_tile")
        zeros = held.tile([P, S], BF16, name="zeros")
        ident = held.tile([P, P], BF16, name="ident")

        for g in range(P // SQ):
            queue = nc.scalar if g % 2 == 0 else nc.sync
            queue.dma_start(c_cols[g * SQ : (g + 1) * SQ, :], c.rearrange("o (q b) -> (o q) b", q=SQ))
        base_blocks = base.rearrange("(h a p) t -> h p a t", h=2, p=P)
        for h in range(2):
            nc.sync.dma_start(halves[h][:], base_blocks[h])
        nc.sync.dma_start(offsets[:], offs)
        nc.sync.dma_start(w_tile[:], w.rearrange("e k m -> k e m"))
        nc.sync.dma_start(x_tile[:], x)
        make_identity(nc, ident[:])
        nc.vector.memset(zeros[:], 0.0)

        idle_bank = psum.tile([P, S], F32, name="idle_bank")
        for step in range(4):
            nc.tensor.matmul(idle_bank[:], zeros[:, :P], zeros[:], start=True, stop=True)

        nc.vector.tensor_copy(c_blocks[:], c_cols[:].unsqueeze(2).to_broadcast([P, S // SQ, SQ]))
        nc.vector.transpose(c_flipped[:], c_blocks[:].rearrange("p b q -> p (b q)"))
        nc.vector.tensor_copy(
            c_tile[:].rearrange("p (q b) -> p q b", q=SQ), c_flipped[:].rearrange("p (b q) -> p q b", q=SQ)
        )

        windows = [psum.tile([P, S], F32, name=f"window{a}") for a in range(blocks)]
        for a in range(blocks):
            nc.tensor.matmul(windows[a][:], ident[:], halves[a // 2][:, a % 2, :], start=True, stop=False)

        for a in range(blocks):
            for e in range(E):
                piece = offsets[:, e * Q // 16 : (e + 1) * Q // 16]
                nc.tensor.matmul(
                    windows[a][:].indirect(piece),
                    w_tile[:, e, a * P : (a + 1) * P],
                    x_tile[:, e * Q : (e + 1) * Q],
                    start=False,
                    stop=(e == E - 1),
                )

        for a in range(blocks):
            result = held.tile([P, S], F32, name=f"result{a}")
            nc.vector.tensor_tensor(result[:], windows[a][:], c_tile[:], mybir.AluOpType.mult)
            nc.sync.dma_start(out[a * P : (a + 1) * P, :], result[:])
